import numpy as np
import ml_dtypes


def mxq(x, axis, fmt="e4m3"):
    dtype, down = {"e4m3": (ml_dtypes.float8_e4m3fn, 7), "e5m2": (ml_dtypes.float8_e5m2, 14)}[fmt]
    v = np.moveaxis(np.asarray(x, np.float32).astype(ml_dtypes.bfloat16).astype(np.float64), axis, -1)
    blocks = v.reshape(v.shape[:-1] + (-1, 32))
    amax = np.abs(blocks).max(-1, keepdims=True)
    byte = np.maximum(np.where(amax > 0, np.frexp(amax)[1] - 1 + 127, 0) - down, 1)
    scale = np.exp2(byte - 127.0)
    codes = (blocks / scale).astype(np.float32).astype(dtype).astype(np.float64)
    return np.moveaxis((codes * scale).reshape(v.shape), -1, axis)


WIDE = False


def mx_kscale(k, group=512):
    if not WIDE:
        return np.ones(k)
    levels = np.array([10, -10, 5, -5, 0])
    if group != 512:
        return np.exp2(np.random.permutation(np.resize(levels, k // group))).repeat(group)
    if k % 512:
        return np.exp2(np.random.permutation(np.resize(levels, k // 32))).repeat(32)
    a = np.empty((k // 512, 16))
    for p in range(k // 512):
        a[p, :8] = np.random.permutation(np.resize(levels, 8))
        for g in range(8):
            far = levels[np.abs(levels - a[p, g]) >= 10]
            a[p, g + 8] = far[np.random.randint(len(far))]
    return np.exp2(a.ravel()).repeat(32)


def f64(x):
    return np.asarray(x).astype(np.float64)


G, D, M, O, N = 2, 256, 128, 256, 512


def setup_inputs():
    n = np.random.standard_normal
    s_d = mx_kscale(D, 0)
    s_o = mx_kscale(O, 0)
    return {
        "x": (n((G, D, N)) * s_d[:, None]).astype(np.float32),
        "w1": (n((G, D, M)) / np.sqrt(D) / s_d[:, None]).astype(np.float32),
        "w2": (n((G, D, M)) / np.sqrt(D) / s_d[:, None]).astype(np.float32),
        "w3": (n((G, D, M)) / np.sqrt(D) / s_d[:, None]).astype(np.float32),
        "wo": (n((G, O, M)) / np.sqrt(O) / s_o[:, None]).astype(np.float32),
        "dy": (n((G, O, N)) * s_o[:, None]).astype(np.float32),
        "dx": (n((G, D, N)) * s_d[:, None]).astype(np.float32),
        "og": (np.random.uniform(0.5, 2.0, (G, M, 1))).astype(np.float32),
        "base": (0.3 * n((G, M, N))).astype(np.float32),
    }


def reference(x, w1, w2, w3, wo, dy, dx, og, base):
    w1q = mxq(f64(w1), 1, "e4m3")
    xq = mxq(f64(x), 1, "e4m3")
    z1 = w1q.transpose(0, 2, 1) @ xq
    dxq = mxq(f64(dx), 1, "e4m3")
    tz1 = w1q.transpose(0, 2, 1) @ dxq
    w2q = mxq(f64(w2), 1, "e4m3")
    z2 = w2q.transpose(0, 2, 1) @ xq
    tz2 = w2q.transpose(0, 2, 1) @ dxq
    w3q = mxq(f64(w3), 1, "e4m3")
    z3 = w3q.transpose(0, 2, 1) @ xq
    tz3 = w3q.transpose(0, 2, 1) @ dxq
    se = np.exp(z1) + np.exp(z2) + np.exp(z3)
    woq = mxq(f64(wo), 1, "e4m3")
    dyq = mxq(f64(dy), 1, "e4m3")
    c0 = woq.transpose(0, 2, 1) @ dyq
    dse = c0 * np.tanh(z1) / se
    xse = tz1 * np.exp(z1) + tz2 * np.exp(z2) + tz3 * np.exp(z3)
    xdse = (tz1 * (1.0 - np.square(np.tanh(z1))) * c0 - xse * c0 * np.tanh(z1) / se) / se
    xdz1 = xse / se * c0 * (1.0 - np.square(np.tanh(z1))) + tz1 * (1.0 - np.square(np.tanh(z1))) * np.tanh(z1) * 2.0 * (-1.0) * c0 * np.log(se) + xdse * np.exp(z1) + tz1 * np.exp(z1) * dse
    y = xdz1 * f64(og) + f64(base)
    return y

@@ -1,0 +1,236 @@
+from contextlib import ExitStack
+
+import concourse.mybir as mybir
+
+G, D, M, N = 2, 256, 128, 512
+FLOPS = 7 * 2 * G * D * M * N
+
+F32 = mybir.dt.float32
+BF16 = mybir.dt.bfloat16
+U32 = mybir.dt.uint32
+U8 = mybir.dt.uint8
+FP8X4 = mybir.dt.float8_e4m3fn_x4
+ACT = mybir.ActivationFunctionType
+ALU = mybir.AluOpType
+
+P = 128
+PACK = 4
+ROWS = D // PACK
+HALF = N // 2
+X_SPLIT = 336
+DX_SPLIT = 352
+
+
+def tile_rows_hvsoftmaxthree_kernel(tc, x, w1, w2, w3, wo, dy, dx, og, base, out):
+    nc = tc.nc
+    with ExitStack() as ctx:
+        sb = ctx.enter_context(tc.tile_pool(name="sb", bufs=1))
+        ps = ctx.enter_context(tc.psum_pool(name="ps", bufs=1))
+        ctx.enter_context(tc.manual_schedule())
+
+        def load(name, src):
+            width = src.shape[2]
+            raw = sb.tile([P, PACK, width], F32, name=name + "_raw")
+            nc.sync.dma_start(out=raw[:], in_=src.rearrange("g (p j) n -> (g p) j n", j=PACK))
+            packed = sb.tile([P, width, PACK], BF16, name=name + "_bf", align_bytes=64)
+            return raw, packed
+
+        def load_halves(name, src):
+            packed = sb.tile([P, N, PACK], BF16, name=name + "_bf", align_bytes=64)
+            parts = []
+            for h in range(2):
+                raw = sb.tile([P, PACK, HALF], F32, name=name + "_raw" + str(h))
+                cols = slice(HALF * h, HALF * (h + 1))
+                nc.sync.dma_start(out=raw[:], in_=src.rearrange("g (p j) n -> (g p) j n", j=PACK)[:, :, cols])
+                parts.append((raw, packed[:, cols, :]))
+            return parts, (None, packed)
+
+        def interleave(copy, operand, cols):
+            raw, packed = operand
+            copy(
+                out=packed[:, cols, :].rearrange("p (c i) j -> p c j i", i=4),
+                in_=raw[:, :, cols].rearrange("p j (c i) -> p c j i", i=4),
+            )
+
+        def quantize(name, operand):
+            packed = operand[1]
+            width = packed.shape[1]
+            codes = sb.tile([P, width], U32, name=name + "_codes", align_bytes=64)
+            scales = sb.tile([P, width], U8, name=name + "_scales", align_bytes=64)
+            nc.vector.quantize_mx(
+                out=codes[:].bitcast(FP8X4), scales=scales[:], in_=packed[:].rearrange("p n j -> p (n j)")
+            )
+            return codes, scales
+
+        def product(banks, weights, moving, groups=range(G)):
+            for g in groups:
+                rows = slice(ROWS * g, ROWS * (g + 1))
+                nc.tensor.matmul_mx(
+                    out=banks[g][:],
+                    lhsT=weights[0][rows, :].bitcast(FP8X4),
+                    lhsT_scale=weights[1][rows, :],
+                    rhs=moving[0][rows, :].bitcast(FP8X4),
+                    rhs_scale=moving[1][rows, :],
+                    start=True,
+                    stop=True,
+                )
+
+        def field(name):
+            return sb.tile([P, G, N], F32, name=name)
+
+        def banks_of(name):
+            return [ps.tile([P, N], F32, name=name + str(g)) for g in range(G)]
+
+        x_in = load("x", x)
+        w2_in = load("w2", w2)
+        w3_in = load("w3", w3)
+        w1_in = load("w1", w1)
+        dx_in = load("dx", dx)
+        wo_in = load("wo", wo)
+        dy_in = load("dy", dy)
+        base_sb = field("base_sb")
+        nc.sync.dma_start(out=base_sb[:], in_=base.rearrange("g m n -> m g n"))
+        gain = []
+        for g in range(G):
+            gain_g = sb.tile([P, 1], F32, name="gain" + str(g))
+            with nc.allow_non_contiguous_dma(reason="one gain a partition"):
+                nc.sync.dma_start(out=gain_g[:], in_=og[g])
+            gain.append(gain_g)
+
+        bank2 = banks_of("bank2")
+        bank3 = banks_of("bank3")
+        z1_ps = banks_of("z1_ps")
+        tz1_ps = banks_of("tz1_ps")
+
+        names = ("e1", "e2", "e3", "s23", "se", "te2", "te3", "ts23", "tsum", "wnum", "lse", "rse", "th", "th2")
+        e1, e2, e3, s23, se, te2, te3, ts23, tsum, wnum, lse, rse, th, th2 = [field(n) for n in names]
+        names = ("p1", "wd", "tl", "kk", "tp", "nsa", "prod", "hh", "wh", "ff", "fc", "res")
+        p1, wd, tl, kk, tp, nsa, prod, hh, wh, ff, fc, res = [field(n) for n in names]
+        every_m = slice(0, M)
+        every_n = slice(0, N)
+
+        def part(t, g, c):
+            return t[g][:, c] if isinstance(t, list) else t[:, g, c]
+
+        def act(dst, src, func, scale=1.0):
+            return lambda g: nc.scalar.activation(out=dst[:, g, :], in_=part(src, g, every_n), func=func, scale=scale)
+
+        def tt(dst, a, b, op, engine=nc.vector):
+            return lambda g, c=every_n: engine.tensor_tensor(
+                out=dst[:, g, c], in0=part(a, g, c), in1=part(b, g, c), op=op
+            )
+
+        def stt(dst, a, s, b, op0, op1):
+            return lambda g, c=every_n: nc.vector.scalar_tensor_tensor(
+                out=dst[:, g, c],
+                in0=part(a, g, c),
+                scalar=s[g][:] if isinstance(s, list) else s,
+                in1=part(b, g, c),
+                op0=op0,
+                op1=op1,
+            )
+
+        def flat(dst, a, b, op, engine, c):
+            view = lambda t: t[:].rearrange("p g n -> p (g n)")[:, c]
+            engine.tensor_tensor(out=view(dst), in0=view(a), in1=view(b), op=op)
+
+        a_e1, a_e2, a_e3 = act(e1, z1_ps, ACT.Exp), act(e2, bank2, ACT.Exp), act(e3, bank3, ACT.Exp)
+        a_lse, a_rse = act(lse, se, ACT.Ln), act(rse, lse, ACT.Exp, -1.0)
+        a_th, a_th2 = act(th, z1_ps, ACT.Tanh), act(th2, th, ACT.Square)
+        v_s23 = tt(s23, e2, e3, ALU.add)
+        v_se = tt(se, s23, e1, ALU.add)
+        g_se = tt(se, s23, e1, ALU.add, nc.gpsimd)
+        v_te2 = tt(te2, bank2, e2, ALU.mult)
+        v_te3 = tt(te3, bank3, e3, ALU.mult)
+        v_ts23 = tt(ts23, tz1_ps, s23, ALU.mult)
+        v_tsum = tt(tsum, te2, te3, ALU.add)
+        g_tsum = tt(tsum, te2, te3, ALU.add, nc.gpsimd)
+        v_wnum = tt(wnum, ts23, tsum, ALU.subtract)
+        v_p1 = tt(p1, e1, rse, ALU.mult)
+        v_wd = tt(wd, wnum, rse, ALU.mult)
+        g_wd = tt(wd, wnum, rse, ALU.mult, nc.gpsimd)
+        v_tl = tt(tl, th, lse, ALU.mult)
+        v_tp = tt(tp, th, p1, ALU.mult)
+        v_kk = stt(kk, tl, -2.0, p1, ALU.mult, ALU.add)
+        v_nsa = stt(nsa, th2, 1.0, tz1_ps, ALU.subtract, ALU.mult)
+        v_hh = stt(hh, th2, 1.0, tp, ALU.subtract, ALU.add)
+        v_prod = stt(prod, kk, 1.0, nsa, ALU.add, ALU.mult)
+        v_wh = tt(wh, wd, hh, ALU.mult)
+        v_ff = tt(ff, wh, prod, ALU.subtract)
+        v_fc = stt(fc, ff, gain, bank2, ALU.mult, ALU.mult)
+        v_add = tt(res, fc, base_sb, ALU.add)
+
+        def v_res(g, c=every_n):
+            v_add(g, c)
+            nc.sync.dma_start(out=out[g, :, c], in_=res[:, g, c])
+
+        interleave(nc.vector.tensor_copy, x_in, slice(0, X_SPLIT))
+        interleave(nc.scalar.copy, x_in, slice(X_SPLIT, N))
+        interleave(nc.scalar.copy, w2_in, every_m)
+        xq = quantize("x", x_in)
+        w2q = quantize("w2", w2_in)
+        product(bank2, w2q, xq)
+        interleave(nc.vector.tensor_copy, w3_in, every_m)
+        interleave(nc.scalar.copy, w1_in, every_m)
+        w3q = quantize("w3", w3_in)
+        product(bank3, w3q, xq)
+        w1q = quantize("w1", w1_in)
+        product(z1_ps, w1q, xq)
+        a_e2(0)
+        a_e2(1)
+        interleave(nc.vector.tensor_copy, dx_in, slice(0, DX_SPLIT))
+        interleave(nc.scalar.copy, dx_in, slice(DX_SPLIT, N))
+        a_e3(0)
+        a_e3(1)
+        a_e1(0)
+        a_e1(1)
+        dxq = quantize("dx", dx_in)
+        for g in range(G):
+            product(bank2, w2q, dxq, [g])
+            product(bank3, w3q, dxq, [g])
+        product(tz1_ps, w1q, dxq)
+        v_s23(0)
+        v_s23(1)
+        v_se(0)
+        v_te2(0)
+        v_se(1)
+        v_te3(0)
+        v_te2(1)
+        v_te3(1)
+        v_ts23(0)
+        v_ts23(1)
+        v_tsum(0)
+        v_tsum(1)
+        v_wnum(0)
+        v_wnum(1)
+        a_lse(0)
+        a_lse(1)
+        for g in range(G):
+            a_rse(g)
+            a_th(g)
+        a_th2(0)
+        a_th2(1)
+        interleave(nc.scalar.copy, wo_in, every_m)
+        interleave(nc.scalar.copy, dy_in, every_n)
+        for g in range(G):
+            v_p1(g)
+            v_wd(g)
+            v_tl(g)
+        for step in (v_tp, v_kk, v_nsa, v_hh):
+            step(0)
+            step(1)
+        woq = quantize("wo", wo_in)
+        dyq = quantize("dy", dy_in)
+        product(bank2, woq, dyq)
+        v_prod(0)
+        v_wh(0)
+        v_prod(1)
+        v_ff(0)
+        v_wh(1)
+        v_fc(0)
+        v_ff(1)
+        v_res(0)
+        halves = (slice(0, HALF), slice(HALF, N))
+        for step in (v_fc, v_res):
+            for c in halves:
+                step(1, c)

@@ -18,7 +18,7 @@ PACK = 4
 ROWS = D // PACK
 HALF = N // 2
 X_SPLIT = 336
-DX_SPLIT = 352
+DX_SPLIT = 384
 
 
 def tile_rows_hvsoftmaxthree_kernel(tc, x, w1, w2, w3, wo, dy, dx, og, base, out):
@@ -173,34 +173,37 @@ def tile_rows_hvsoftmaxthree_kernel(tc, x, w1, w2, w3, wo, dy, dx, og, base, out
         interleave(nc.vector.tensor_copy, w3_in, every_m)
         interleave(nc.scalar.copy, w1_in, every_m)
         w3q = quantize("w3", w3_in)
-        product(bank3, w3q, xq)
+        product(bank3, w3q, xq, [0])
         w1q = quantize("w1", w1_in)
-        product(z1_ps, w1q, xq)
+        product(z1_ps, w1q, xq, [0])
+        product(bank3, w3q, xq, [1])
+        product(z1_ps, w1q, xq, [1])
         a_e2(0)
         a_e2(1)
+        a_e3(0)
         interleave(nc.vector.tensor_copy, dx_in, slice(0, DX_SPLIT))
         interleave(nc.scalar.copy, dx_in, slice(DX_SPLIT, N))
-        a_e3(0)
-        a_e3(1)
+        v_s23(0)
         a_e1(0)
+        a_e3(1)
         a_e1(1)
         dxq = quantize("dx", dx_in)
         for g in range(G):
             product(bank2, w2q, dxq, [g])
             product(bank3, w3q, dxq, [g])
         product(tz1_ps, w1q, dxq)
-        v_s23(0)
-        v_s23(1)
         v_se(0)
+        v_s23(1)
+        g_se(1)
         v_te2(0)
-        v_se(1)
         v_te3(0)
+        g_tsum(0)
         v_te2(1)
         v_te3(1)
+        flat(tsum, te2, te3, ALU.add, nc.gpsimd, slice(N, N + 256))
         v_ts23(0)
         v_ts23(1)
-        v_tsum(0)
-        v_tsum(1)
+        flat(tsum, te2, te3, ALU.add, nc.vector, slice(N + 256, 2 * N))
         v_wnum(0)
         v_wnum(1)
         a_lse(0)
@@ -216,21 +219,26 @@ def tile_rows_hvsoftmaxthree_kernel(tc, x, w1, w2, w3, wo, dy, dx, og, base, out
             v_p1(g)
             v_wd(g)
             v_tl(g)
-        for step in (v_tp, v_kk, v_nsa, v_hh):
+        for step in (v_tp, v_kk):
             step(0)
             step(1)
+        v_hh(1)
+        v_hh(0)
+        flat(wh, wd, hh, ALU.mult, nc.gpsimd, slice(0, 384))
+        v_nsa(0)
+        v_nsa(1)
         woq = quantize("wo", wo_in)
         dyq = quantize("dy", dy_in)
         product(bank2, woq, dyq)
         v_prod(0)
-        v_wh(0)
+        flat(wh, wd, hh, ALU.mult, nc.vector, slice(384, 2 * N))
         v_prod(1)
         v_ff(0)
-        v_wh(1)
-        v_fc(0)
         v_ff(1)
-        v_res(0)
+        v_fc(0)
         halves = (slice(0, HALF), slice(HALF, N))
-        for step in (v_fc, v_res):
-            for c in halves:
-                step(1, c)
+        v_fc(1, halves[0])
+        v_res(0)
+        v_fc(1, halves[1])
+        v_res(1, halves[0])
+        v_res(1, halves[1])

@@ -62,6 +62,19 @@ def tile_rows_hvsoftmaxthree_kernel(tc, x, w1, w2, w3, wo, dy, dx, og, base, out
             )
             return codes, scales
 
+        def planes(name):
+            codes = sb.tile([P, N], U32, name=name + "_codes", align_bytes=64)
+            scales = sb.tile([P, N], U8, name=name + "_scales", align_bytes=64)
+            return codes, scales
+
+        def quantize_half(q, operand, h):
+            cols = slice(HALF * h, HALF * (h + 1))
+            nc.vector.quantize_mx(
+                out=q[0][:, cols].bitcast(FP8X4),
+                scales=q[1][:, cols],
+                in_=operand[1][:, cols, :].rearrange("p n j -> p (n j)"),
+            )
+
         def product(banks, weights, moving, groups=range(G)):
             for g in groups:
                 rows = slice(ROWS * g, ROWS * (g + 1))
@@ -85,7 +98,7 @@ def tile_rows_hvsoftmaxthree_kernel(tc, x, w1, w2, w3, wo, dy, dx, og, base, out
         w2_in = load("w2", w2)
         w3_in = load("w3", w3)
         w1_in = load("w1", w1)
-        dx_in = load("dx", dx)
+        dx_parts, dx_in = load_halves("dx", dx)
         wo_in = load("wo", wo)
         dy_in = load("dy", dy)
         base_sb = field("base_sb")
@@ -137,6 +150,9 @@ def tile_rows_hvsoftmaxthree_kernel(tc, x, w1, w2, w3, wo, dy, dx, og, base, out
         a_e1, a_e2, a_e3 = act(e1, z1_ps, ACT.Exp), act(e2, bank2, ACT.Exp), act(e3, bank3, ACT.Exp)
         a_lse, a_rse = act(lse, se, ACT.Ln), act(rse, lse, ACT.Exp, -1.0)
         a_th, a_th2 = act(th, z1_ps, ACT.Tanh), act(th2, th, ACT.Square)
+        lp1 = field("lp1")
+        v_lp1 = tt(lp1, z1_ps, lse, ALU.subtract)
+        a_p1 = act(p1, lp1, ACT.Exp)
         v_s23 = tt(s23, e2, e3, ALU.add)
         v_se = tt(se, s23, e1, ALU.add)
         g_se = tt(se, s23, e1, ALU.add, nc.gpsimd)
@@ -173,65 +189,65 @@ def tile_rows_hvsoftmaxthree_kernel(tc, x, w1, w2, w3, wo, dy, dx, og, base, out
         interleave(nc.vector.tensor_copy, w3_in, every_m)
         interleave(nc.scalar.copy, w1_in, every_m)
         w3q = quantize("w3", w3_in)
-        product(bank3, w3q, xq, [0])
+        product(bank3, w3q, xq)
         w1q = quantize("w1", w1_in)
-        product(z1_ps, w1q, xq, [0])
-        product(bank3, w3q, xq, [1])
-        product(z1_ps, w1q, xq, [1])
+        product(z1_ps, w1q, xq)
         a_e2(0)
         a_e2(1)
         a_e3(0)
-        interleave(nc.vector.tensor_copy, dx_in, slice(0, DX_SPLIT))
-        interleave(nc.scalar.copy, dx_in, slice(DX_SPLIT, N))
-        v_s23(0)
-        a_e1(0)
         a_e3(1)
+        a_e1(0)
         a_e1(1)
-        dxq = quantize("dx", dx_in)
+        dxq = planes("dx")
+        interleave(nc.vector.tensor_copy, dx_parts[0], slice(0, HALF))
+        quantize_half(dxq, dx_in, 0)
+        interleave(nc.vector.tensor_copy, dx_parts[1], slice(0, HALF))
+        v_s23(0)
+        quantize_half(dxq, dx_in, 1)
         for g in range(G):
             product(bank2, w2q, dxq, [g])
             product(bank3, w3q, dxq, [g])
         product(tz1_ps, w1q, dxq)
-        v_se(0)
         v_s23(1)
+        v_se(0)
         g_se(1)
+        a_lse(0)
+        a_lse(1)
         v_te2(0)
         v_te3(0)
         g_tsum(0)
         v_te2(1)
         v_te3(1)
-        flat(tsum, te2, te3, ALU.add, nc.gpsimd, slice(N, N + 256))
+        g_tsum(1)
         v_ts23(0)
+        flat(wnum, ts23, tsum, ALU.subtract, nc.gpsimd, slice(0, 160))
         v_ts23(1)
-        flat(tsum, te2, te3, ALU.add, nc.vector, slice(N + 256, 2 * N))
-        v_wnum(0)
-        v_wnum(1)
-        a_lse(0)
-        a_lse(1)
+        v_lp1(0)
+        v_lp1(1)
+        flat(wnum, ts23, tsum, ALU.subtract, nc.vector, slice(160, 2 * N))
         for g in range(G):
-            a_rse(g)
             a_th(g)
+            a_rse(g)
+            a_p1(g)
         a_th2(0)
         a_th2(1)
         interleave(nc.scalar.copy, wo_in, every_m)
         interleave(nc.scalar.copy, dy_in, every_n)
         for g in range(G):
-            v_p1(g)
-            v_wd(g)
             v_tl(g)
-        for step in (v_tp, v_kk):
-            step(0)
-            step(1)
+            v_wd(g)
+            v_tp(g)
+            v_kk(g)
         v_hh(1)
         v_hh(0)
         flat(wh, wd, hh, ALU.mult, nc.gpsimd, slice(0, 384))
         v_nsa(0)
         v_nsa(1)
+        v_prod(0)
+        flat(wh, wd, hh, ALU.mult, nc.vector, slice(384, 2 * N))
         woq = quantize("wo", wo_in)
         dyq = quantize("dy", dy_in)
         product(bank2, woq, dyq)
-        v_prod(0)
-        flat(wh, wd, hh, ALU.mult, nc.vector, slice(384, 2 * N))
         v_prod(1)
         v_ff(0)
         v_ff(1)

@@ -16,77 +16,60 @@ ALU = mybir.AluOpType
 P = 128
 PACK = 4
 ROWS = D // PACK
+RUN = 4
 HALF = N // 2
-X_SPLIT = 336
-DX_SPLIT = 384
+X_ON_VECTOR = 336
+NUMERATOR_ON_GPSIMD = 160
+PRODUCT_ON_GPSIMD = 384
 
 
 def tile_rows_hvsoftmaxthree_kernel(tc, x, w1, w2, w3, wo, dy, dx, og, base, out):
     nc = tc.nc
+    every_m = slice(0, M)
+    every_n = slice(0, N)
+    halves = (slice(0, HALF), slice(HALF, N))
+
     with ExitStack() as ctx:
         sb = ctx.enter_context(tc.tile_pool(name="sb", bufs=1))
         ps = ctx.enter_context(tc.psum_pool(name="ps", bufs=1))
         ctx.enter_context(tc.manual_schedule())
 
-        def load(name, src):
-            width = src.shape[2]
-            raw = sb.tile([P, PACK, width], F32, name=name + "_raw")
-            nc.sync.dma_start(out=raw[:], in_=src.rearrange("g (p j) n -> (g p) j n", j=PACK))
-            packed = sb.tile([P, width, PACK], BF16, name=name + "_bf", align_bytes=64)
-            return raw, packed
+        def load(name, src, cols):
+            raw = sb.tile([P, PACK, cols.stop - cols.start], F32, name=name + "_raw")
+            nc.sync.dma_start(out=raw[:], in_=src.rearrange("g (p j) n -> (g p) j n", j=PACK)[:, :, cols])
+            return raw
 
-        def load_halves(name, src):
-            packed = sb.tile([P, N, PACK], BF16, name=name + "_bf", align_bytes=64)
-            parts = []
-            for h in range(2):
-                raw = sb.tile([P, PACK, HALF], F32, name=name + "_raw" + str(h))
-                cols = slice(HALF * h, HALF * (h + 1))
-                nc.sync.dma_start(out=raw[:], in_=src.rearrange("g (p j) n -> (g p) j n", j=PACK)[:, :, cols])
-                parts.append((raw, packed[:, cols, :]))
-            return parts, (None, packed)
-
-        def interleave(copy, operand, cols):
-            raw, packed = operand
-            copy(
-                out=packed[:, cols, :].rearrange("p (c i) j -> p c j i", i=4),
-                in_=raw[:, :, cols].rearrange("p j (c i) -> p c j i", i=4),
-            )
-
-        def quantize(name, operand):
-            packed = operand[1]
-            width = packed.shape[1]
+        def operand(name, width):
+            values = sb.tile([P, width, PACK], BF16, name=name + "_values", align_bytes=64)
             codes = sb.tile([P, width], U32, name=name + "_codes", align_bytes=64)
             scales = sb.tile([P, width], U8, name=name + "_scales", align_bytes=64)
-            nc.vector.quantize_mx(
-                out=codes[:].bitcast(FP8X4), scales=scales[:], in_=packed[:].rearrange("p n j -> p (n j)")
-            )
-            return codes, scales
+            return values, codes, scales
 
-        def planes(name):
-            codes = sb.tile([P, N], U32, name=name + "_codes", align_bytes=64)
-            scales = sb.tile([P, N], U8, name=name + "_scales", align_bytes=64)
-            return codes, scales
-
-        def quantize_half(q, operand, h):
-            cols = slice(HALF * h, HALF * (h + 1))
-            nc.vector.quantize_mx(
-                out=q[0][:, cols].bitcast(FP8X4),
-                scales=q[1][:, cols],
-                in_=operand[1][:, cols, :].rearrange("p n j -> p (n j)"),
+        def interleave(copy, mx, cols, raw_cols):
+            copy(
+                out=mx[0][:, cols, :].rearrange("p (c i) j -> p c j i", i=RUN),
+                in_=raw_cols.rearrange("p j (c i) -> p c j i", i=RUN),
             )
 
-        def product(banks, weights, moving, groups=range(G)):
-            for g in groups:
-                rows = slice(ROWS * g, ROWS * (g + 1))
-                nc.tensor.matmul_mx(
-                    out=banks[g][:],
-                    lhsT=weights[0][rows, :].bitcast(FP8X4),
-                    lhsT_scale=weights[1][rows, :],
-                    rhs=moving[0][rows, :].bitcast(FP8X4),
-                    rhs_scale=moving[1][rows, :],
-                    start=True,
-                    stop=True,
-                )
+        def quantize(mx, cols):
+            values, codes, scales = mx
+            nc.vector.quantize_mx(
+                out=codes[:, cols].bitcast(FP8X4),
+                scales=scales[:, cols],
+                in_=values[:, cols, :].rearrange("p n j -> p (n j)"),
+            )
+
+        def product(banks, weights, moving, g):
+            rows = slice(ROWS * g, ROWS * (g + 1))
+            nc.tensor.matmul_mx(
+                out=banks[g][:],
+                lhsT=weights[1][rows, :].bitcast(FP8X4),
+                lhsT_scale=weights[2][rows, :],
+                rhs=moving[1][rows, :].bitcast(FP8X4),
+                rhs_scale=moving[2][rows, :],
+                start=True,
+                stop=True,
+            )
 
         def field(name):
             return sb.tile([P, G, N], F32, name=name)
@@ -94,13 +77,16 @@ def tile_rows_hvsoftmaxthree_kernel(tc, x, w1, w2, w3, wo, dy, dx, og, base, out
         def banks_of(name):
             return [ps.tile([P, N], F32, name=name + str(g)) for g in range(G)]
 
-        x_in = load("x", x)
-        w2_in = load("w2", w2)
-        w3_in = load("w3", w3)
-        w1_in = load("w1", w1)
-        dx_parts, dx_in = load_halves("dx", dx)
-        wo_in = load("wo", wo)
-        dy_in = load("dy", dy)
+        def flat(tile, cols):
+            return tile[:].rearrange("p g n -> p (g n)")[:, cols]
+
+        x_raw = load("x", x, every_n)
+        w2_raw = load("w2", w2, every_m)
+        w3_raw = load("w3", w3, every_m)
+        w1_raw = load("w1", w1, every_m)
+        dx_raw = [load("dx" + str(h), dx, halves[h]) for h in range(2)]
+        wo_raw = load("wo", wo, every_m)
+        dy_raw = load("dy", dy, every_n)
         base_sb = field("base_sb")
         nc.sync.dma_start(out=base_sb[:], in_=base.rearrange("g m n -> m g n"))
         gain = []
@@ -110,151 +96,153 @@ def tile_rows_hvsoftmaxthree_kernel(tc, x, w1, w2, w3, wo, dy, dx, og, base, out
                 nc.sync.dma_start(out=gain_g[:], in_=og[g])
             gain.append(gain_g)
 
-        bank2 = banks_of("bank2")
-        bank3 = banks_of("bank3")
+        x_mx, dx_mx, dy_mx = operand("x", N), operand("dx", N), operand("dy", N)
+        w1_mx, w2_mx, w3_mx, wo_mx = operand("w1", M), operand("w2", M), operand("w3", M), operand("wo", M)
+
+        second_ps = banks_of("second_ps")
+        third_ps = banks_of("third_ps")
         z1_ps = banks_of("z1_ps")
         tz1_ps = banks_of("tz1_ps")
 
-        names = ("e1", "e2", "e3", "s23", "se", "te2", "te3", "ts23", "tsum", "wnum", "lse", "rse", "th", "th2")
-        e1, e2, e3, s23, se, te2, te3, ts23, tsum, wnum, lse, rse, th, th2 = [field(n) for n in names]
-        names = ("p1", "wd", "tl", "kk", "tp", "nsa", "prod", "hh", "wh", "ff", "fc", "res")
-        p1, wd, tl, kk, tp, nsa, prod, hh, wh, ff, fc, res = [field(n) for n in names]
-        every_m = slice(0, M)
-        every_n = slice(0, N)
+        e1, e2, e3, e23, se, lse = [field(n) for n in ("e1", "e2", "e3", "e23", "se", "lse")]
+        tz2_e2, tz3_e3, tz_e23, tz1_e23 = [field(n) for n in ("tz2_e2", "tz3_e3", "tz_e23", "tz1_e23")]
+        numerator, log_p1, inv_se, p1 = [field(n) for n in ("numerator", "log_p1", "inv_se", "p1")]
+        th, th_sq, th_lse, th_p1, dev = [field(n) for n in ("th", "th_sq", "th_lse", "th_p1", "dev")]
+        factor, bracket, neg_tz1_s, neg_first = [field(n) for n in ("factor", "bracket", "neg_tz1_s", "neg_first")]
+        second, total, scaled, result = [field(n) for n in ("second", "total", "scaled", "result")]
 
-        def part(t, g, c):
-            return t[g][:, c] if isinstance(t, list) else t[:, g, c]
+        interleave(nc.vector.tensor_copy, x_mx, slice(0, X_ON_VECTOR), x_raw[:, :, :X_ON_VECTOR])
+        interleave(nc.scalar.copy, x_mx, slice(X_ON_VECTOR, N), x_raw[:, :, X_ON_VECTOR:])
+        interleave(nc.scalar.copy, w2_mx, every_m, w2_raw[:])
+        quantize(x_mx, every_n)
+        quantize(w2_mx, every_m)
+        interleave(nc.vector.tensor_copy, w3_mx, every_m, w3_raw[:])
+        interleave(nc.scalar.copy, w1_mx, every_m, w1_raw[:])
+        quantize(w3_mx, every_m)
+        quantize(w1_mx, every_m)
+        for banks, weights, e in ((second_ps, w2_mx, e2), (third_ps, w3_mx, e3), (z1_ps, w1_mx, e1)):
+            for g in range(G):
+                product(banks, weights, x_mx, g)
+                nc.scalar.activation(out=e[:, g, :], in_=banks[g][:], func=ACT.Exp)
 
-        def act(dst, src, func, scale=1.0):
-            return lambda g: nc.scalar.activation(out=dst[:, g, :], in_=part(src, g, every_n), func=func, scale=scale)
+        def add_e23(g):
+            nc.vector.tensor_tensor(out=e23[:, g, :], in0=e2[:, g, :], in1=e3[:, g, :], op=ALU.add)
 
-        def tt(dst, a, b, op, engine=nc.vector):
-            return lambda g, c=every_n: engine.tensor_tensor(
-                out=dst[:, g, c], in0=part(a, g, c), in1=part(b, g, c), op=op
+        def add_se(engine, g):
+            engine.tensor_tensor(out=se[:, g, :], in0=e23[:, g, :], in1=e1[:, g, :], op=ALU.add)
+
+        interleave(nc.vector.tensor_copy, dx_mx, halves[0], dx_raw[0][:])
+        quantize(dx_mx, halves[0])
+        interleave(nc.vector.tensor_copy, dx_mx, halves[1], dx_raw[1][:])
+        add_e23(0)
+        quantize(dx_mx, halves[1])
+        for g in range(G):
+            product(second_ps, w2_mx, dx_mx, g)
+            product(third_ps, w3_mx, dx_mx, g)
+        for g in range(G):
+            product(tz1_ps, w1_mx, dx_mx, g)
+        add_e23(1)
+        add_se(nc.vector, 0)
+        add_se(nc.gpsimd, 1)
+        for g in range(G):
+            nc.scalar.activation(out=lse[:, g, :], in_=se[:, g, :], func=ACT.Ln)
+
+        def mul_tz1_e23(g):
+            nc.vector.tensor_tensor(out=tz1_e23[:, g, :], in0=tz1_ps[g][:], in1=e23[:, g, :], op=ALU.mult)
+
+        def sub_numerator(engine, cols):
+            engine.tensor_tensor(
+                out=flat(numerator, cols), in0=flat(tz1_e23, cols), in1=flat(tz_e23, cols), op=ALU.subtract
             )
 
-        def stt(dst, a, s, b, op0, op1):
-            return lambda g, c=every_n: nc.vector.scalar_tensor_tensor(
-                out=dst[:, g, c],
-                in0=part(a, g, c),
-                scalar=s[g][:] if isinstance(s, list) else s,
-                in1=part(b, g, c),
-                op0=op0,
-                op1=op1,
+        for g in range(G):
+            nc.vector.tensor_tensor(out=tz2_e2[:, g, :], in0=second_ps[g][:], in1=e2[:, g, :], op=ALU.mult)
+            nc.vector.tensor_tensor(out=tz3_e3[:, g, :], in0=third_ps[g][:], in1=e3[:, g, :], op=ALU.mult)
+            nc.gpsimd.tensor_tensor(out=tz_e23[:, g, :], in0=tz2_e2[:, g, :], in1=tz3_e3[:, g, :], op=ALU.add)
+        mul_tz1_e23(0)
+        sub_numerator(nc.gpsimd, slice(0, NUMERATOR_ON_GPSIMD))
+        for g in range(G):
+            nc.vector.tensor_tensor(out=log_p1[:, g, :], in0=z1_ps[g][:], in1=lse[:, g, :], op=ALU.subtract)
+        mul_tz1_e23(1)
+        sub_numerator(nc.vector, slice(NUMERATOR_ON_GPSIMD, N))
+        sub_numerator(nc.vector, slice(N, G * N))
+
+        for g in range(G):
+            nc.scalar.activation(out=th[:, g, :], in_=z1_ps[g][:], func=ACT.Tanh)
+            nc.scalar.activation(out=inv_se[:, g, :], in_=lse[:, g, :], func=ACT.Exp, scale=-1.0)
+            nc.scalar.activation(out=p1[:, g, :], in_=log_p1[:, g, :], func=ACT.Exp)
+        for g in range(G):
+            nc.scalar.activation(out=th_sq[:, g, :], in_=th[:, g, :], func=ACT.Square)
+        interleave(nc.scalar.copy, wo_mx, every_m, wo_raw[:])
+        interleave(nc.scalar.copy, dy_mx, every_n, dy_raw[:])
+
+        for g in range(G):
+            nc.vector.tensor_tensor(out=th_lse[:, g, :], in0=th[:, g, :], in1=lse[:, g, :], op=ALU.mult)
+            nc.vector.tensor_tensor(out=dev[:, g, :], in0=numerator[:, g, :], in1=inv_se[:, g, :], op=ALU.mult)
+            nc.vector.tensor_tensor(out=th_p1[:, g, :], in0=th[:, g, :], in1=p1[:, g, :], op=ALU.mult)
+        both = slice(0, G * N)
+        nc.vector.scalar_tensor_tensor(
+            out=flat(factor, both), in0=flat(th_lse, both), scalar=-2.0, in1=flat(p1, both), op0=ALU.mult, op1=ALU.add
+        )
+        nc.vector.scalar_tensor_tensor(
+            out=flat(bracket, both),
+            in0=flat(th_sq, both),
+            scalar=1.0,
+            in1=flat(th_p1, both),
+            op0=ALU.subtract,
+            op1=ALU.add,
+        )
+
+        def mul_second(engine, cols):
+            engine.tensor_tensor(out=flat(second, cols), in0=flat(dev, cols), in1=flat(bracket, cols), op=ALU.mult)
+
+        def mul_neg_first(g):
+            nc.vector.scalar_tensor_tensor(
+                out=neg_first[:, g, :],
+                in0=factor[:, g, :],
+                scalar=1.0,
+                in1=neg_tz1_s[:, g, :],
+                op0=ALU.add,
+                op1=ALU.mult,
             )
 
-        def flat(dst, a, b, op, engine, c):
-            view = lambda t: t[:].rearrange("p g n -> p (g n)")[:, c]
-            engine.tensor_tensor(out=view(dst), in0=view(a), in1=view(b), op=op)
-
-        a_e1, a_e2, a_e3 = act(e1, z1_ps, ACT.Exp), act(e2, bank2, ACT.Exp), act(e3, bank3, ACT.Exp)
-        a_lse, a_rse = act(lse, se, ACT.Ln), act(rse, lse, ACT.Exp, -1.0)
-        a_th, a_th2 = act(th, z1_ps, ACT.Tanh), act(th2, th, ACT.Square)
-        lp1 = field("lp1")
-        v_lp1 = tt(lp1, z1_ps, lse, ALU.subtract)
-        a_p1 = act(p1, lp1, ACT.Exp)
-        v_s23 = tt(s23, e2, e3, ALU.add)
-        v_se = tt(se, s23, e1, ALU.add)
-        g_se = tt(se, s23, e1, ALU.add, nc.gpsimd)
-        v_te2 = tt(te2, bank2, e2, ALU.mult)
-        v_te3 = tt(te3, bank3, e3, ALU.mult)
-        v_ts23 = tt(ts23, tz1_ps, s23, ALU.mult)
-        v_tsum = tt(tsum, te2, te3, ALU.add)
-        g_tsum = tt(tsum, te2, te3, ALU.add, nc.gpsimd)
-        v_wnum = tt(wnum, ts23, tsum, ALU.subtract)
-        v_p1 = tt(p1, e1, rse, ALU.mult)
-        v_wd = tt(wd, wnum, rse, ALU.mult)
-        g_wd = tt(wd, wnum, rse, ALU.mult, nc.gpsimd)
-        v_tl = tt(tl, th, lse, ALU.mult)
-        v_tp = tt(tp, th, p1, ALU.mult)
-        v_kk = stt(kk, tl, -2.0, p1, ALU.mult, ALU.add)
-        v_nsa = stt(nsa, th2, 1.0, tz1_ps, ALU.subtract, ALU.mult)
-        v_hh = stt(hh, th2, 1.0, tp, ALU.subtract, ALU.add)
-        v_prod = stt(prod, kk, 1.0, nsa, ALU.add, ALU.mult)
-        v_wh = tt(wh, wd, hh, ALU.mult)
-        v_ff = tt(ff, wh, prod, ALU.subtract)
-        v_fc = stt(fc, ff, gain, bank2, ALU.mult, ALU.mult)
-        v_add = tt(res, fc, base_sb, ALU.add)
-
-        def v_res(g, c=every_n):
-            v_add(g, c)
-            nc.sync.dma_start(out=out[g, :, c], in_=res[:, g, c])
-
-        interleave(nc.vector.tensor_copy, x_in, slice(0, X_SPLIT))
-        interleave(nc.scalar.copy, x_in, slice(X_SPLIT, N))
-        interleave(nc.scalar.copy, w2_in, every_m)
-        xq = quantize("x", x_in)
-        w2q = quantize("w2", w2_in)
-        product(bank2, w2q, xq)
-        interleave(nc.vector.tensor_copy, w3_in, every_m)
-        interleave(nc.scalar.copy, w1_in, every_m)
-        w3q = quantize("w3", w3_in)
-        product(bank3, w3q, xq)
-        w1q = quantize("w1", w1_in)
-        product(z1_ps, w1q, xq)
-        a_e2(0)
-        a_e2(1)
-        a_e3(0)
-        a_e3(1)
-        a_e1(0)
-        a_e1(1)
-        dxq = planes("dx")
-        interleave(nc.vector.tensor_copy, dx_parts[0], slice(0, HALF))
-        quantize_half(dxq, dx_in, 0)
-        interleave(nc.vector.tensor_copy, dx_parts[1], slice(0, HALF))
-        v_s23(0)
-        quantize_half(dxq, dx_in, 1)
+        mul_second(nc.gpsimd, slice(0, PRODUCT_ON_GPSIMD))
         for g in range(G):
-            product(bank2, w2q, dxq, [g])
-            product(bank3, w3q, dxq, [g])
-        product(tz1_ps, w1q, dxq)
-        v_s23(1)
-        v_se(0)
-        g_se(1)
-        a_lse(0)
-        a_lse(1)
-        v_te2(0)
-        v_te3(0)
-        g_tsum(0)
-        v_te2(1)
-        v_te3(1)
-        g_tsum(1)
-        v_ts23(0)
-        flat(wnum, ts23, tsum, ALU.subtract, nc.gpsimd, slice(0, 160))
-        v_ts23(1)
-        v_lp1(0)
-        v_lp1(1)
-        flat(wnum, ts23, tsum, ALU.subtract, nc.vector, slice(160, 2 * N))
+            nc.vector.scalar_tensor_tensor(
+                out=neg_tz1_s[:, g, :],
+                in0=th_sq[:, g, :],
+                scalar=1.0,
+                in1=tz1_ps[g][:],
+                op0=ALU.subtract,
+                op1=ALU.mult,
+            )
+        mul_neg_first(0)
+        mul_second(nc.vector, slice(PRODUCT_ON_GPSIMD, G * N))
+        quantize(wo_mx, every_m)
+        quantize(dy_mx, every_n)
         for g in range(G):
-            a_th(g)
-            a_rse(g)
-            a_p1(g)
-        a_th2(0)
-        a_th2(1)
-        interleave(nc.scalar.copy, wo_in, every_m)
-        interleave(nc.scalar.copy, dy_in, every_n)
+            product(second_ps, wo_mx, dy_mx, g)
+        mul_neg_first(1)
         for g in range(G):
-            v_tl(g)
-            v_wd(g)
-            v_tp(g)
-            v_kk(g)
-        v_hh(1)
-        v_hh(0)
-        flat(wh, wd, hh, ALU.mult, nc.gpsimd, slice(0, 384))
-        v_nsa(0)
-        v_nsa(1)
-        v_prod(0)
-        flat(wh, wd, hh, ALU.mult, nc.vector, slice(384, 2 * N))
-        woq = quantize("wo", wo_in)
-        dyq = quantize("dy", dy_in)
-        product(bank2, woq, dyq)
-        v_prod(1)
-        v_ff(0)
-        v_ff(1)
-        v_fc(0)
-        halves = (slice(0, HALF), slice(HALF, N))
-        v_fc(1, halves[0])
-        v_res(0)
-        v_fc(1, halves[1])
-        v_res(1, halves[0])
-        v_res(1, halves[1])
+            nc.vector.tensor_tensor(out=total[:, g, :], in0=second[:, g, :], in1=neg_first[:, g, :], op=ALU.subtract)
+
+        def scale_by_c0(g, cols):
+            nc.vector.scalar_tensor_tensor(
+                out=scaled[:, g, cols],
+                in0=total[:, g, cols],
+                scalar=gain[g][:],
+                in1=second_ps[g][:, cols],
+                op0=ALU.mult,
+                op1=ALU.mult,
+            )
+
+        def add_base_and_store(g, cols):
+            nc.vector.tensor_tensor(out=result[:, g, cols], in0=scaled[:, g, cols], in1=base_sb[:, g, cols], op=ALU.add)
+            nc.sync.dma_start(out=out[g, :, cols], in_=result[:, g, cols])
+
+        scale_by_c0(0, every_n)
+        scale_by_c0(1, halves[0])
+        add_base_and_store(0, every_n)
+        scale_by_c0(1, halves[1])
+        add_base_and_store(1, halves[0])
+        add_base_and_store(1, halves[1])

from contextlib import ExitStack

import concourse.mybir as mybir

G, D, M, N = 2, 256, 128, 512
FLOPS = 7 * 2 * G * D * M * N

F32 = mybir.dt.float32
BF16 = mybir.dt.bfloat16
U32 = mybir.dt.uint32
U8 = mybir.dt.uint8
FP8X4 = mybir.dt.float8_e4m3fn_x4
ACT = mybir.ActivationFunctionType
ALU = mybir.AluOpType

P = 128
PACK = 4
ROWS = D // PACK
RUN = 4
HALF = N // 2
X_ON_VECTOR = 336
NUMERATOR_ON_GPSIMD = 160
PRODUCT_ON_GPSIMD = 384


def tile_rows_hvsoftmaxthree_kernel(tc, x, w1, w2, w3, wo, dy, dx, og, base, out):
    nc = tc.nc
    every_m = slice(0, M)
    every_n = slice(0, N)
    halves = (slice(0, HALF), slice(HALF, N))

    with ExitStack() as ctx:
        sb = ctx.enter_context(tc.tile_pool(name="sb", bufs=1))
        ps = ctx.enter_context(tc.psum_pool(name="ps", bufs=1))
        ctx.enter_context(tc.manual_schedule())

        def load(name, src, cols):
            raw = sb.tile([P, PACK, cols.stop - cols.start], F32, name=name + "_raw")
            nc.sync.dma_start(out=raw[:], in_=src.rearrange("g (p j) n -> (g p) j n", j=PACK)[:, :, cols])
            return raw

        def operand(name, width):
            values = sb.tile([P, width, PACK], BF16, name=name + "_values", align_bytes=64)
            codes = sb.tile([P, width], U32, name=name + "_codes", align_bytes=64)
            scales = sb.tile([P, width], U8, name=name + "_scales", align_bytes=64)
            return values, codes, scales

        def interleave(copy, mx, cols, raw_cols):
            copy(
                out=mx[0][:, cols, :].rearrange("p (c i) j -> p c j i", i=RUN),
                in_=raw_cols.rearrange("p j (c i) -> p c j i", i=RUN),
            )

        def quantize(mx, cols):
            values, codes, scales = mx
            nc.vector.quantize_mx(
                out=codes[:, cols].bitcast(FP8X4),
                scales=scales[:, cols],
                in_=values[:, cols, :].rearrange("p n j -> p (n j)"),
            )

        def product(banks, weights, moving, g):
            rows = slice(ROWS * g, ROWS * (g + 1))
            nc.tensor.matmul_mx(
                out=banks[g][:],
                lhsT=weights[1][rows, :].bitcast(FP8X4),
                lhsT_scale=weights[2][rows, :],
                rhs=moving[1][rows, :].bitcast(FP8X4),
                rhs_scale=moving[2][rows, :],
                start=True,
                stop=True,
            )

        def field(name):
            return sb.tile([P, G, N], F32, name=name)

        def banks_of(name):
            return [ps.tile([P, N], F32, name=name + str(g)) for g in range(G)]

        def flat(tile, cols):
            return tile[:].rearrange("p g n -> p (g n)")[:, cols]

        x_raw = load("x", x, every_n)
        w2_raw = load("w2", w2, every_m)
        w3_raw = load("w3", w3, every_m)
        w1_raw = load("w1", w1, every_m)
        dx_raw = [load("dx" + str(h), dx, halves[h]) for h in range(2)]
        wo_raw = load("wo", wo, every_m)
        dy_raw = load("dy", dy, every_n)
        base_sb = field("base_sb")
        nc.sync.dma_start(out=base_sb[:], in_=base.rearrange("g m n -> m g n"))
        gain = []
        for g in range(G):
            gain_g = sb.tile([P, 1], F32, name="gain" + str(g))
            with nc.allow_non_contiguous_dma(reason="one gain a partition"):
                nc.sync.dma_start(out=gain_g[:], in_=og[g])
            gain.append(gain_g)

        x_mx, dx_mx, dy_mx = operand("x", N), operand("dx", N), operand("dy", N)
        w1_mx, w2_mx, w3_mx, wo_mx = operand("w1", M), operand("w2", M), operand("w3", M), operand("wo", M)

        second_ps = banks_of("second_ps")
        third_ps = banks_of("third_ps")
        z1_ps = banks_of("z1_ps")
        tz1_ps = banks_of("tz1_ps")

        e1, e2, e3, e23, se, lse = [field(n) for n in ("e1", "e2", "e3", "e23", "se", "lse")]
        tz2_e2, tz3_e3, tz_e23, tz1_e23 = [field(n) for n in ("tz2_e2", "tz3_e3", "tz_e23", "tz1_e23")]
        numerator, log_p1, inv_se, p1 = [field(n) for n in ("numerator", "log_p1", "inv_se", "p1")]
        th, th_sq, th_lse, th_p1, dev = [field(n) for n in ("th", "th_sq", "th_lse", "th_p1", "dev")]
        factor, bracket, neg_tz1_s, neg_first = [field(n) for n in ("factor", "bracket", "neg_tz1_s", "neg_first")]
        second, total, scaled, result = [field(n) for n in ("second", "total", "scaled", "result")]

        interleave(nc.vector.tensor_copy, x_mx, slice(0, X_ON_VECTOR), x_raw[:, :, :X_ON_VECTOR])
        interleave(nc.scalar.copy, x_mx, slice(X_ON_VECTOR, N), x_raw[:, :, X_ON_VECTOR:])
        interleave(nc.scalar.copy, w2_mx, every_m, w2_raw[:])
        quantize(x_mx, every_n)
        quantize(w2_mx, every_m)
        interleave(nc.vector.tensor_copy, w3_mx, every_m, w3_raw[:])
        interleave(nc.scalar.copy, w1_mx, every_m, w1_raw[:])
        quantize(w3_mx, every_m)
        quantize(w1_mx, every_m)
        for banks, weights, e in ((second_ps, w2_mx, e2), (third_ps, w3_mx, e3), (z1_ps, w1_mx, e1)):
            for g in range(G):
                product(banks, weights, x_mx, g)
                nc.scalar.activation(out=e[:, g, :], in_=banks[g][:], func=ACT.Exp)

        def add_e23(g):
            nc.vector.tensor_tensor(out=e23[:, g, :], in0=e2[:, g, :], in1=e3[:, g, :], op=ALU.add)

        def add_se(engine, g):
            engine.tensor_tensor(out=se[:, g, :], in0=e23[:, g, :], in1=e1[:, g, :], op=ALU.add)

        interleave(nc.vector.tensor_copy, dx_mx, halves[0], dx_raw[0][:])
        quantize(dx_mx, halves[0])
        interleave(nc.vector.tensor_copy, dx_mx, halves[1], dx_raw[1][:])
        add_e23(0)
        quantize(dx_mx, halves[1])
        for g in range(G):
            product(second_ps, w2_mx, dx_mx, g)
            product(third_ps, w3_mx, dx_mx, g)
        for g in range(G):
            product(tz1_ps, w1_mx, dx_mx, g)
        add_e23(1)
        add_se(nc.vector, 0)
        add_se(nc.gpsimd, 1)
        for g in range(G):
            nc.scalar.activation(out=lse[:, g, :], in_=se[:, g, :], func=ACT.Ln)

        def mul_tz1_e23(g):
            nc.vector.tensor_tensor(out=tz1_e23[:, g, :], in0=tz1_ps[g][:], in1=e23[:, g, :], op=ALU.mult)

        def sub_numerator(engine, cols):
            engine.tensor_tensor(
                out=flat(numerator, cols), in0=flat(tz1_e23, cols), in1=flat(tz_e23, cols), op=ALU.subtract
            )

        for g in range(G):
            nc.vector.tensor_tensor(out=tz2_e2[:, g, :], in0=second_ps[g][:], in1=e2[:, g, :], op=ALU.mult)
            nc.vector.tensor_tensor(out=tz3_e3[:, g, :], in0=third_ps[g][:], in1=e3[:, g, :], op=ALU.mult)
            nc.gpsimd.tensor_tensor(out=tz_e23[:, g, :], in0=tz2_e2[:, g, :], in1=tz3_e3[:, g, :], op=ALU.add)
        mul_tz1_e23(0)
        sub_numerator(nc.gpsimd, slice(0, NUMERATOR_ON_GPSIMD))
        for g in range(G):
            nc.vector.tensor_tensor(out=log_p1[:, g, :], in0=z1_ps[g][:], in1=lse[:, g, :], op=ALU.subtract)
        mul_tz1_e23(1)
        sub_numerator(nc.vector, slice(NUMERATOR_ON_GPSIMD, N))
        sub_numerator(nc.vector, slice(N, G * N))

        for g in range(G):
            nc.scalar.activation(out=th[:, g, :], in_=z1_ps[g][:], func=ACT.Tanh)
            nc.scalar.activation(out=inv_se[:, g, :], in_=lse[:, g, :], func=ACT.Exp, scale=-1.0)
            nc.scalar.activation(out=p1[:, g, :], in_=log_p1[:, g, :], func=ACT.Exp)
        for g in range(G):
            nc.scalar.activation(out=th_sq[:, g, :], in_=th[:, g, :], func=ACT.Square)
        interleave(nc.scalar.copy, wo_mx, every_m, wo_raw[:])
        interleave(nc.scalar.copy, dy_mx, every_n, dy_raw[:])

        for g in range(G):
            nc.vector.tensor_tensor(out=th_lse[:, g, :], in0=th[:, g, :], in1=lse[:, g, :], op=ALU.mult)
            nc.vector.tensor_tensor(out=dev[:, g, :], in0=numerator[:, g, :], in1=inv_se[:, g, :], op=ALU.mult)
            nc.vector.tensor_tensor(out=th_p1[:, g, :], in0=th[:, g, :], in1=p1[:, g, :], op=ALU.mult)
        both = slice(0, G * N)
        nc.vector.scalar_tensor_tensor(
            out=flat(factor, both), in0=flat(th_lse, both), scalar=-2.0, in1=flat(p1, both), op0=ALU.mult, op1=ALU.add
        )
        nc.vector.scalar_tensor_tensor(
            out=flat(bracket, both),
            in0=flat(th_sq, both),
            scalar=1.0,
            in1=flat(th_p1, both),
            op0=ALU.subtract,
            op1=ALU.add,
        )

        def mul_second(engine, cols):
            engine.tensor_tensor(out=flat(second, cols), in0=flat(dev, cols), in1=flat(bracket, cols), op=ALU.mult)

        def mul_neg_first(g):
            nc.vector.scalar_tensor_tensor(
                out=neg_first[:, g, :],
                in0=factor[:, g, :],
                scalar=1.0,
                in1=neg_tz1_s[:, g, :],
                op0=ALU.add,
                op1=ALU.mult,
            )

        mul_second(nc.gpsimd, slice(0, PRODUCT_ON_GPSIMD))
        for g in range(G):
            nc.vector.scalar_tensor_tensor(
                out=neg_tz1_s[:, g, :],
                in0=th_sq[:, g, :],
                scalar=1.0,
                in1=tz1_ps[g][:],
                op0=ALU.subtract,
                op1=ALU.mult,
            )
        mul_neg_first(0)
        mul_second(nc.vector, slice(PRODUCT_ON_GPSIMD, G * N))
        quantize(wo_mx, every_m)
        quantize(dy_mx, every_n)
        for g in range(G):
            product(second_ps, wo_mx, dy_mx, g)
        mul_neg_first(1)
        for g in range(G):
            nc.vector.tensor_tensor(out=total[:, g, :], in0=second[:, g, :], in1=neg_first[:, g, :], op=ALU.subtract)

        def scale_by_c0(g, cols):
            nc.vector.scalar_tensor_tensor(
                out=scaled[:, g, cols],
                in0=total[:, g, cols],
                scalar=gain[g][:],
                in1=second_ps[g][:, cols],
                op0=ALU.mult,
                op1=ALU.mult,
            )

        def add_base_and_store(g, cols):
            nc.vector.tensor_tensor(out=result[:, g, cols], in0=scaled[:, g, cols], in1=base_sb[:, g, cols], op=ALU.add)
            nc.sync.dma_start(out=out[g, :, cols], in_=result[:, g, cols])

        scale_by_c0(0, every_n)
        scale_by_c0(1, halves[0])
        add_base_and_store(0, every_n)
        scale_by_c0(1, halves[1])
        add_base_and_store(1, halves[0])
        add_base_and_store(1, halves[1])
